import numpy as np
import ml_dtypes


def mxq(x, axis, fmt="e4m3"):
    dtype, down = {"e4m3": (ml_dtypes.float8_e4m3fn, 7), "e5m2": (ml_dtypes.float8_e5m2, 14)}[fmt]
    v = np.moveaxis(np.asarray(x, np.float32).astype(ml_dtypes.bfloat16).astype(np.float64), axis, -1)
    blocks = v.reshape(v.shape[:-1] + (-1, 32))
    amax = np.abs(blocks).max(-1, keepdims=True)
    byte = np.maximum(np.where(amax > 0, np.frexp(amax)[1] - 1 + 127, 0) - down, 1)
    scale = np.exp2(byte - 127.0)
    codes = (blocks / scale).astype(np.float32).astype(dtype).astype(np.float64)
    return np.moveaxis((codes * scale).reshape(v.shape), -1, axis)


WIDE = False


def mx_kscale(k):
    if not WIDE:
        return np.ones(k)
    levels = np.array([10, -10, 5, -5, 0])
    if k % 512:
        return np.exp2(np.random.permutation(np.resize(levels, k // 32))).repeat(32)
    a = np.empty((k // 512, 16))
    for p in range(k // 512):
        a[p, :8] = np.random.permutation(np.resize(levels, 8))
        for g in range(8):
            far = levels[np.abs(levels - a[p, g]) >= 10]
            a[p, g + 8] = far[np.random.randint(len(far))]
    return np.exp2(a.ravel()).repeat(32)


BF16 = ml_dtypes.bfloat16


def bf(x):
    return np.asarray(x, np.float32).astype(BF16)


def f64(x):
    return np.asarray(x).astype(np.float64)


R, S, P, F, C = 128, 8, 3, 256, 1024
F2 = 2 * F


def draw0():
    s, t = mx_kscale(F2), mx_kscale(C)
    n = np.random.standard_normal((P, F))
    freq = 3.1 * n / np.abs(n).sum(axis=0)
    return {
        "pos": bf(np.random.uniform(-1.0, 1.0, (R, S, P))),
        "dt": bf(np.random.uniform(0.1, 0.5, (R, S))),
        "freq": bf(freq),
        "g": bf((1.0 + 0.2 * np.random.standard_normal(F2)) * s),
        "w1": bf(np.random.standard_normal((F2, C)) * 1.4 / np.sqrt(F2) / s[:, None] * t),
        "ws": bf(np.random.standard_normal((F2, C)) / np.sqrt(F2) / s[:, None] * t),
        "w2": bf(np.random.standard_normal((C, C)) * 1.5 / np.sqrt(C) / t[:, None]),
    }


def fourier_encode(pos, freq, g):
    ph = pos[..., 0:1] * freq[0] + pos[..., 1:2] * freq[1] + pos[..., 2:3] * freq[2]
    return g * np.concatenate([np.sin(ph), np.cos(ph)], axis=-1)


def softplus(u):
    return np.maximum(u, 0.0) + np.log(1.0 + np.exp(-np.abs(u)))


def sigmoid(u):
    return 1.0 / (1.0 + np.exp(-u))


def exclusive_sum(a):
    before = [np.zeros_like(a[:, 0])]
    for s in range(1, a.shape[1]):
        before.append(before[-1] + a[:, s - 1])
    return np.stack(before, axis=1)


def core(pos, dt, freq, g, w1, ws, w2):
    e = fourier_encode(f64(pos), f64(freq), f64(g))
    eq = mxq(e, 2, "e4m3")

    h = np.maximum(eq @ mxq(f64(w1), 0, "e4m3"), 0.0) + (eq @ mxq(f64(ws), 0, "e4m3"))

    o = mxq(h, 2, "e4m3") @ mxq(f64(w2), 0, "e4m3")

    sigma = softplus(o[..., 0])
    a = sigma * f64(dt)

    wgt = np.exp(-exclusive_sum(a)) * (1.0 - np.exp(-a))

    return np.sum(wgt[..., None] * sigmoid(o), axis=1)


def e4m3fn_bytes(y):
    return np.clip(np.asarray(y, np.float64), -448.0, 448.0).astype(np.float32).astype(ml_dtypes.float8_e4m3fn).view(np.uint8)


def e4m3fn_values(b):
    return np.asarray(b, np.uint8).view(ml_dtypes.float8_e4m3fn).astype(np.float64)


def setup_inputs():
    d = draw0()
    x0 = np.asarray(d['w2']).astype(np.float64)
    s = (np.max(np.abs(x0), axis=(1,), keepdims=True) / 448.0).astype(np.float32)
    out = {}
    for k, v in d.items():
        if k == 'w2':
            out['w2_bytes'] = e4m3fn_bytes(x0 / s.astype(np.float64))
            out['w2_scale'] = s
        else:
            out[k] = v
    return out


def reference(pos, dt, freq, g, w1, ws, w2_bytes, w2_scale):
    return core(pos, dt, freq, g, w1, ws, e4m3fn_values(w2_bytes) * w2_scale.astype(np.float64))

@@ -1,0 +1,449 @@
+import math
+from contextlib import ExitStack
+
+import concourse.mybir as mybir
+from concourse.masks import make_identity
+
+R, S, F, F2, C = 128, 8, 256, 512, 1024
+P = 128
+PACK = 4
+G = 2
+CG = 512
+NB = 4
+FLOPS = 2 * R * S * (2 * F2 * C + C * C)
+
+F32 = mybir.dt.float32
+BF16 = mybir.dt.bfloat16
+U32 = mybir.dt.uint32
+U8 = mybir.dt.uint8
+FP8 = mybir.dt.float8_e4m3fn
+FP8X4 = mybir.dt.float8_e4m3fn_x4
+ACT = mybir.ActivationFunctionType
+ALU = mybir.AluOpType
+
+
+def tile_fouriernerffeaturerenderer_kernel(tc, pos, dt, freq, g, w1, ws, w2_bytes, w2_scale, out):
+    nc = tc.nc
+    with ExitStack() as ctx:
+        keep = ctx.enter_context(tc.tile_pool(name="keep", bufs=1))
+        work = ctx.enter_context(tc.tile_pool(name="work", bufs=2))
+        psum = ctx.enter_context(tc.psum_pool(name="psum", bufs=8))
+        ctx.enter_context(tc.manual_schedule())
+
+        def bank(shape, dtype, name):
+            return psum.tile(shape, dtype, name=name, tag="bank", bufs=8)
+
+        fr = keep.tile([P, F2], BF16, name="fr")
+        nc.vector.memset(fr[:], 0.0)
+        pb = keep.tile([P, S, P], BF16, name="pb")
+        nc.gpsimd.memset(pb[:], 0.0)
+        posr = keep.tile([P, S, 3], BF16, name="posr")
+        nc.sync.dma_start(out=posr[:], in_=pos)
+        for h in range(2):
+            nc.scalar.dma_start(out=fr[0:3, h * F : (h + 1) * F], in_=freq)
+        g4 = keep.tile([P, PACK], BF16, name="g4")
+        nc.scalar.dma_start(out=g4[:], in_=g.rearrange("(p t) -> p t", t=PACK))
+        w2s = keep.tile([P, G, PACK], F32, name="w2s")
+        nc.scalar.dma_start(out=w2s[:], in_=w2_scale.rearrange("(g p t) o -> p g (t o)", p=P, t=PACK))
+        dtb = keep.tile([P, S], BF16, name="dtb")
+        nc.scalar.dma_start(out=dtb[:], in_=dt)
+
+        raw = {}
+        w2b = {}
+        for gi in range(G):
+            for br, src in enumerate((w1, ws)):
+                t_raw = keep.tile([P, PACK, CG], BF16, name="raw%d%d" % (gi, br))
+                view = src.rearrange("(p j) c -> p j c", j=PACK)
+                parts = 2 if (gi, br) == (0, 0) else 1
+                for h in range(parts):
+                    w = CG // parts
+                    nc.sync.dma_start(
+                        out=t_raw[:, :, h * w : (h + 1) * w], in_=view[:, :, gi * CG + h * w : gi * CG + (h + 1) * w]
+                    )
+                raw[gi, br] = t_raw
+                if br == 1:
+                    t_b = keep.tile([P, PACK, C], U8, name="w2b%d" % gi)
+                    nc.sync.dma_start(out=t_b[:], in_=w2_bytes.rearrange("(g p t) n -> g p t n", p=P, t=PACK)[gi])
+                    w2b[gi] = t_b
+
+        ident = keep.tile([P, P], BF16, name="ident")
+        make_identity(nc, ident[:])
+
+        sgn = keep.tile([P, 1], F32, name="sgn")
+        nc.vector.memset(sgn[0:64], -1.0)
+        nc.vector.memset(sgn[64:128], 0.0)
+        shift = keep.tile([P, 1], F32, name="shift")
+        nc.vector.tensor_scalar(out=shift[:], in0=sgn[:], scalar1=math.pi / 2, scalar2=None, op0=ALU.mult)
+        one = keep.tile([P, S], F32, name="one")
+        nc.vector.memset(one[:], 1.0)
+        hpi = keep.tile([P, 1], F32, name="hpi")
+        nc.vector.tensor_scalar(out=hpi[:], in0=one[:, 0:1], scalar1=math.pi / 2, scalar2=None, op0=ALU.mult)
+        base = keep.tile([P, 2, S], F32, name="base")
+        nc.vector.tensor_scalar(out=base[:, 1, :], in0=one[:], scalar1=1.0 / math.e, scalar2=None, op0=ALU.mult)
+        expo = keep.tile([P, 2, S], F32, name="expo")
+        trans = keep.tile([P, S + 1], F32, name="trans")
+        nc.vector.memset(trans[:, 0:1], 1.0)
+        warm = keep.tile([P, 1], F32, name="warm")
+        nc.scalar.activation(out=warm[:], in_=sgn[:], func=ACT.Sin)
+
+        post = keep.tile([P, S, P], BF16, name="post")
+        state = {}
+
+        def pos_place():
+            nc.vector.tensor_copy(out=pb[:, :, 0:3], in_=posr[:])
+
+        def pos_turn():
+            t = bank([P, S, P], BF16, "pos_ps")
+            for s in range(S):
+                nc.tensor.transpose(t[:, s, :], pb[:, s, :], ident[:])
+            state["pos"] = t
+
+        def pos_copy():
+            nc.scalar.copy(out=post[:], in_=state["pos"][:])
+
+        wi, wq, wsc = {}, {}, {}
+
+        def w_lay(gi, br, h):
+            if h == 0:
+                wi[gi, br] = work.tile([P, CG * PACK], BF16, name="wi", bufs=3, align_bytes=64)
+            m = slice(h * 64, (h + 1) * 64)
+            nc.vector.tensor_copy(
+                out=wi[gi, br][:].rearrange("p (t m j) -> p t m j", t=PACK, j=PACK)[:, :, m, :],
+                in_=raw[gi, br][:].rearrange("p j (m t) -> p t m j", t=PACK)[:, :, m, :],
+            )
+
+        def w_lay_s(gi, br, h):
+            if h == 0:
+                wi[gi, br] = work.tile([P, CG * PACK], BF16, name="wi", bufs=3, align_bytes=64)
+            m = slice(h * 64, (h + 1) * 64)
+            nc.scalar.copy(
+                out=wi[gi, br][:].rearrange("p (t m j) -> p t m j", t=PACK, j=PACK)[:, :, m, :],
+                in_=raw[gi, br][:].rearrange("p j (m t) -> p t m j", t=PACK)[:, :, m, :],
+            )
+
+        def w_quant(gi, br):
+            codes = keep.tile([P, CG], U32, name="wq%d%d" % (gi, br), align_bytes=64)
+            scales = keep.tile([P, CG], U8, name="wsc%d%d" % (gi, br), align_bytes=64)
+            nc.vector.quantize_mx(out=codes[:].bitcast(FP8X4), scales=scales[:], in_=wi[gi, br][:])
+            wq[gi, br], wsc[gi, br] = codes, scales
+
+        ph, absx, ysin = {}, {}, {}
+
+        def phase_mm(s):
+            ph[s] = bank([P, PACK, P], F32, "ph")
+            for t in range(PACK):
+                nc.tensor.matmul(out=ph[s][:, t, :], lhsT=fr[:, t::PACK], rhs=post[:, s, :], start=True, stop=True)
+
+        def encode_abs(s):
+            if s % 2 == 0:
+                absx[s // 2] = work.tile([P, 2, P, PACK], F32, name="absx")
+            nc.scalar.activation(
+                out=absx[s // 2][:, s % 2], in_=ph[s][:].rearrange("p t n -> p n t"), func=ACT.Abs, bias=shift[:]
+            )
+
+        def encode_sin(j):
+            ysin[j] = work.tile([P, 2 * P, PACK], F32, name="y")
+            nc.scalar.activation(
+                out=ysin[j][:], in_=absx[j][:].rearrange("p s n t -> p (s n) t"), func=ACT.Sin, bias=hpi[:], scale=-1.0
+            )
+
+        ei, eq, esc = {}, {}, {}
+
+        def encode_mul(j):
+            ei[j] = work.tile([P, 2 * P, PACK], BF16, name="ei", align_bytes=64)
+            nc.vector.tensor_tensor(
+                out=ei[j][:], in0=ysin[j][:], in1=g4[:].unsqueeze(1).to_broadcast([P, 2 * P, PACK]), op=ALU.mult
+            )
+
+        def encode_quant(j):
+            codes = keep.tile([P, 2 * P], U32, name="eq%d" % j, align_bytes=64)
+            scales = keep.tile([P, 2 * P], U8, name="esc%d" % j, align_bytes=64)
+            nc.vector.quantize_mx(
+                out=codes[:].bitcast(FP8X4), scales=scales[:], in_=ei[j][:].rearrange("p n t -> p (n t)")
+            )
+            eq[j], esc[j] = codes, scales
+
+        hi, hq, hsc = {}, {}, {}
+        bank_a, bank_b, relu_a = {}, {}, {}
+
+        def hidden_mm(s, gi, br, name):
+            cols = slice((s % 2) * P, (s % 2 + 1) * P)
+            t_bank = bank([P, PACK, P], F32, name)
+            for t in range(PACK):
+                m = slice(t * P, (t + 1) * P)
+                nc.tensor.matmul_mx(
+                    out=t_bank[:, t, :],
+                    lhsT=wq[gi, br][:, m].bitcast(FP8X4),
+                    lhsT_scale=wsc[gi, br][:, m],
+                    rhs=eq[s // 2][:, cols].bitcast(FP8X4),
+                    rhs_scale=esc[s // 2][:, cols],
+                    start=True,
+                    stop=True,
+                )
+            return t_bank
+
+        def mm_a(s, gi):
+            bank_a[s, gi] = hidden_mm(s, gi, 0, "ba")
+
+        def mm_b(s, gi):
+            bank_b[s, gi] = hidden_mm(s, gi, 1, "bb")
+
+        def relu(s, gi):
+            relu_a[s, gi] = work.tile([P, P, PACK], F32, name="relu", bufs=8)
+            nc.scalar.activation(
+                out=relu_a[s, gi][:], in_=bank_a[s, gi][:].rearrange("p t n -> p n t"), func=ACT.Relu
+            )
+
+        def add(s, gi):
+            if gi == 0:
+                hi[s] = work.tile([P, G, P, PACK], BF16, name="hi", bufs=2, align_bytes=64)
+            nc.vector.tensor_tensor(
+                out=hi[s][:, gi], in0=bank_b[s, gi][:].rearrange("p t n -> p n t"), in1=relu_a[s, gi][:], op=ALU.add
+            )
+
+        def h_quant(s):
+            codes = keep.tile([P, G * P], U32, name="hq%d" % s, align_bytes=64)
+            scales = keep.tile([P, G * P], U8, name="hsc%d" % s, align_bytes=64)
+            nc.vector.quantize_mx(
+                out=codes[:].bitcast(FP8X4), scales=scales[:], in_=hi[s][:].rearrange("p g n t -> p (g n t)")
+            )
+            hq[s], hsc[s] = codes, scales
+
+        w2w, w2i, w2ps = {}, {}, {}
+        w2q, w2sc = {}, {}
+
+        def w2_wide(gi):
+            if gi not in w2w:
+                w2w[gi] = keep.tile([P, PACK, C], BF16, name="w2w%d" % gi)
+            return w2w[gi]
+
+        def widen_s(gi, t):
+            nc.scalar.activation(
+                out=w2_wide(gi)[:, t, :], in_=w2b[gi][:, t, :].bitcast(FP8), func=ACT.Copy, scale=w2s[:, gi, t : t + 1]
+            )
+
+        def widen_v(gi, t):
+            nc.vector.tensor_scalar(
+                out=w2_wide(gi)[:, t, :],
+                in0=w2b[gi][:, t, :].bitcast(FP8),
+                scalar1=w2s[:, gi, t : t + 1],
+                scalar2=None,
+                op0=ALU.mult,
+            )
+
+        def lay(gi, c, h):
+            t_bank = bank([P, 2 * P, PACK], BF16, "lay")
+            for q in range(2):
+                n0 = c * CG + h * 2 * P + q * P
+                nc.tensor.matmul(
+                    out=t_bank[:, q * P : (q + 1) * P, :],
+                    lhsT=ident[:],
+                    rhs=w2w[gi][:, :, n0 : n0 + P].rearrange("p t c -> p c t"),
+                    start=True,
+                    stop=True,
+                )
+            w2ps[gi, c, h] = t_bank
+
+        def lay_copy(gi, c, h):
+            if h == 0:
+                w2i[gi, c] = work.tile([P, CG, PACK], BF16, name="w2i", bufs=4, align_bytes=64)
+            nc.scalar.copy(out=w2i[gi, c][:, h * 2 * P : (h + 1) * 2 * P, :], in_=w2ps[gi, c, h][:])
+
+        def lay_copy_v(gi, c, h):
+            if h == 0:
+                w2i[gi, c] = work.tile([P, CG, PACK], BF16, name="w2i", bufs=4, align_bytes=64)
+            nc.vector.tensor_copy(out=w2i[gi, c][:, h * 2 * P : (h + 1) * 2 * P, :], in_=w2ps[gi, c, h][:])
+
+        def lay_direct(gi, c):
+            w2i[gi, c] = work.tile([P, CG, PACK], BF16, name="w2i", bufs=4, align_bytes=64)
+            nc.vector.tensor_copy(
+                out=w2i[gi, c][:], in_=w2w[gi][:, :, c * CG : (c + 1) * CG].rearrange("p t c -> p c t")
+            )
+
+        def w2_quant(gi, c):
+            codes = keep.tile([P, CG], U32, name="w2q%d%d" % (gi, c), align_bytes=64)
+            scales = keep.tile([P, CG], U8, name="w2sc%d%d" % (gi, c), align_bytes=64)
+            nc.vector.quantize_mx(
+                out=codes[:].bitcast(FP8X4), scales=scales[:], in_=w2i[gi, c][:].rearrange("p c t -> p (c t)")
+            )
+            w2q[gi, c], w2sc[gi, c] = codes, scales
+
+        absu = keep.tile([P, S], F32, name="absu")
+        powr = keep.tile([P, 2, S], F32, name="powr")
+        quot = keep.tile([P, S], F32, name="quot")
+        wgt = keep.tile([P, S], F32, name="wgt")
+
+        def out_mm(dst, s, gi, c, width):
+            m = slice(gi * P, (gi + 1) * P)
+            nc.tensor.matmul_mx(
+                out=dst,
+                lhsT=hq[s][:, m].bitcast(FP8X4),
+                lhsT_scale=hsc[s][:, m],
+                rhs=w2q[gi, c][:, 0:width].bitcast(FP8X4),
+                rhs_scale=w2sc[gi, c][:, 0:width],
+                start=(gi == 0),
+                stop=(gi == G - 1),
+            )
+
+        u_ps, o_ps, sgm = {}, {}, {}
+
+        def u_mm(b):
+            u_ps[b] = bank([P, NB, P], F32, "u_ps")
+            for k in range(NB):
+                for gi in range(G):
+                    out_mm(u_ps[b][:, k, :], b * NB + k, gi, 0, P)
+
+        def batch(b):
+            return slice(b * NB, (b + 1) * NB)
+
+        def den_a(b):
+            if b == 0:
+                nc.vector.tensor_copy(out=expo[:, 0, :], in_=dtb[:])
+            nc.vector.scalar_tensor_tensor(
+                out=expo[:, 1, batch(b)],
+                in0=u_ps[b][:, :, 0],
+                scalar=0.0,
+                in1=dtb[:, batch(b)],
+                op0=ALU.max,
+                op1=ALU.mult,
+            )
+
+        def den_b(b):
+            nc.scalar.activation(out=absu[:, batch(b)], in_=u_ps[b][:, :, 0], func=ACT.Abs)
+            nc.scalar.activation(out=base[:, 0, batch(b)], in_=absu[:, batch(b)], func=ACT.Sigmoid)
+
+        def den_c(b):
+            q = batch(b)
+            nc.gpsimd.tensor_tensor(out=powr[:, :, q], in0=base[:, :, q], in1=expo[:, :, q], op=ALU.pow)
+            nc.gpsimd.tensor_tensor(out=quot[:, q], in0=powr[:, 0, q], in1=powr[:, 1, q], op=ALU.mult)
+
+        def den_d(b):
+            q = batch(b)
+            nxt = slice(b * NB + 1, (b + 1) * NB + 1)
+            nc.vector.tensor_tensor_scan(
+                out=trans[:, nxt],
+                data0=quot[:, q],
+                data1=one[:, q],
+                initial=trans[:, b * NB : b * NB + 1],
+                op0=ALU.mult,
+                op1=ALU.mult,
+            )
+            nc.vector.tensor_tensor(out=wgt[:, q], in0=trans[:, q], in1=trans[:, nxt], op=ALU.subtract)
+
+        def o_mm(s, c):
+            o_ps[s, c] = bank([P, CG], F32, "o_ps")
+            for gi in range(G):
+                out_mm(o_ps[s, c][:], s, gi, c, CG)
+
+        def sig(s, c):
+            sgm[s, c] = work.tile([P, CG], F32, name="sgm", bufs=12)
+            nc.scalar.activation(out=sgm[s, c][:], in_=o_ps[s, c][:], func=ACT.Sigmoid)
+
+        acc = {}
+
+        def comp(s, c):
+            t = work.tile([P, CG], F32, name="acc%d" % c)
+            if s == 0:
+                nc.vector.tensor_scalar(
+                    out=t[:], in0=sgm[s, c][:], scalar1=wgt[:, s : s + 1], scalar2=None, op0=ALU.mult
+                )
+            else:
+                nc.vector.scalar_tensor_tensor(
+                    out=t[:], in0=sgm[s, c][:], scalar=wgt[:, s : s + 1], in1=acc[c][:], op0=ALU.mult, op1=ALU.add
+                )
+            acc[c] = t
+            if s == S - 1:
+                nc.sync.dma_start(out=out[:, c * CG : (c + 1) * CG], in_=acc[c][:])
+
+        pos_place()
+        pos_turn()
+        pos_copy()
+        for s in range(8):
+            phase_mm(s)
+        def encode_s(j):
+            encode_abs(2 * j)
+            encode_abs(2 * j + 1)
+            encode_sin(j)
+        def encode_v(j):
+            encode_mul(j)
+            encode_quant(j)
+        def w2_place(gi):
+            for c in range(2):
+                for h in range(2):
+                    lay(gi, c, h)
+                    lay_copy(gi, c, h)
+        pairs = [(s, gi) for s in range(8) for gi in range(2)]
+        outs = [(s, c) for s in range(8) for c in range(2)]
+        def gate(i):
+            mm_a(*pairs[i])
+            relu(*pairs[i])
+        encode_s(0)
+        w_lay(0, 0, 0)
+        w_lay(0, 0, 1)
+        w_lay(0, 1, 0)
+        w_lay(0, 1, 1)
+        w_quant(0, 0)
+        encode_s(1)
+        for t in range(4):
+            widen_v(0, t)
+        encode_v(0)
+        encode_s(2)
+        w_lay(1, 0, 0)
+        w_lay(1, 0, 1)
+        encode_v(1)
+        widen_s(1, 0)
+        w_quant(0, 1)
+        encode_s(3)
+        widen_v(1, 2)
+        widen_v(1, 3)
+        encode_v(2)
+        w2_place(0)
+        widen_s(1, 1)
+        w_quant(1, 0)
+        gate(0)
+        gate(1)
+        gate(2)
+        gate(3)
+        w_lay(1, 1, 0)
+        w_lay(1, 1, 1)
+        encode_v(3)
+        w_quant(1, 1)
+        w2_place(1)
+        w2_quant(0, 0)
+        w2_quant(0, 1)
+        gate(4)
+        gate(5)
+        mm_b(*pairs[0])
+        mm_b(*pairs[1])
+        for i in range(16):
+            if i + 6 < 16:
+                gate(i + 6)
+            if i + 2 < 16:
+                mm_b(*pairs[i + 2])
+            add(*pairs[i])
+            if i % 2:
+                h_quant(i // 2)
+            if i in (1, 3):
+                w2_quant(1, i // 2)
+            if i == 7:
+                u_mm(0)
+                den_a(0)
+                den_b(0)
+                den_c(0)
+            if i == 12:
+                den_d(0)
+            if i >= 8:
+                o_mm(*outs[i - 8])
+                sig(*outs[i - 8])
+        u_mm(1)
+        for i in range(16):
+            if i + 8 < 16:
+                o_mm(*outs[i + 8])
+                sig(*outs[i + 8])
+            comp(*outs[i])
+            if i == 1:
+                den_a(1)
+                den_b(1)
+                den_c(1)
+            if i == 7:
+                den_d(1)

@@ -48,23 +48,28 @@ def tile_fouriernerffeaturerenderer_kernel(tc, pos, dt, freq, g, w1, ws, w2_byte
         dtb = keep.tile([P, S], BF16, name="dtb")
         nc.scalar.dma_start(out=dtb[:], in_=dt)
 
-        raw = {}
-        w2b = {}
+        raw, w2b = {}, {}
         for gi in range(G):
-            for br, src in enumerate((w1, ws)):
-                t_raw = keep.tile([P, PACK, CG], BF16, name="raw%d%d" % (gi, br))
-                view = src.rearrange("(p j) c -> p j c", j=PACK)
-                parts = 2 if (gi, br) == (0, 0) else 1
-                for h in range(parts):
-                    w = CG // parts
-                    nc.sync.dma_start(
-                        out=t_raw[:, :, h * w : (h + 1) * w], in_=view[:, :, gi * CG + h * w : gi * CG + (h + 1) * w]
-                    )
-                raw[gi, br] = t_raw
-                if br == 1:
-                    t_b = keep.tile([P, PACK, C], U8, name="w2b%d" % gi)
-                    nc.sync.dma_start(out=t_b[:], in_=w2_bytes.rearrange("(g p t) n -> g p t n", p=P, t=PACK)[gi])
-                    w2b[gi] = t_b
+            for br in range(2):
+                raw[gi, br] = keep.tile([P, PACK, CG], BF16, name="raw%d%d" % (gi, br))
+            w2b[gi] = keep.tile([P, PACK, C], U8, name="w2b%d" % gi)
+        w2_view = w2_bytes.rearrange("(g p t) n -> g p t n", p=P, t=PACK)
+        w_view = [src.rearrange("(p j) c -> p j c", j=PACK) for src in (w1, ws)]
+
+        def load_w(gi, br, c0, c1):
+            nc.sync.dma_start(out=raw[gi, br][:, :, c0:c1], in_=w_view[br][:, :, gi * CG + c0 : gi * CG + c1])
+
+        def load_w2(gi, t0, t1):
+            nc.sync.dma_start(out=w2b[gi][:, t0:t1, :], in_=w2_view[gi][:, t0:t1, :])
+
+        load_w2(0, 0, 2)
+        load_w(0, 0, 0, CG // 2)
+        load_w(0, 0, CG // 2, CG)
+        load_w(0, 1, 0, CG)
+        load_w2(0, 2, 4)
+        load_w(1, 0, 0, CG)
+        load_w(1, 1, 0, CG)
+        load_w2(1, 0, 4)
 
         ident = keep.tile([P, P], BF16, name="ident")
         make_identity(nc, ident[:])
@@ -92,14 +97,14 @@ def tile_fouriernerffeaturerenderer_kernel(tc, pos, dt, freq, g, w1, ws, w2_byte
         def pos_place():
             nc.vector.tensor_copy(out=pb[:, :, 0:3], in_=posr[:])
 
-        def pos_turn():
-            t = bank([P, S, P], BF16, "pos_ps")
-            for s in range(S):
-                nc.tensor.transpose(t[:, s, :], pb[:, s, :], ident[:])
-            state["pos"] = t
+        def pos_turn(h):
+            t = bank([P, S // 2, P], BF16, "pos_ps")
+            for s in range(S // 2):
+                nc.tensor.transpose(t[:, s, :], pb[:, h * (S // 2) + s, :], ident[:])
+            state[h] = t
 
-        def pos_copy():
-            nc.scalar.copy(out=post[:], in_=state["pos"][:])
+        def pos_copy(h):
+            nc.scalar.copy(out=post[:, h * (S // 2) : (h + 1) * (S // 2), :], in_=state[h][:])
 
         wi, wq, wsc = {}, {}, {}
 
@@ -136,13 +141,13 @@ def tile_fouriernerffeaturerenderer_kernel(tc, pos, dt, freq, g, w1, ws, w2_byte
 
         def encode_abs(s):
             if s % 2 == 0:
-                absx[s // 2] = work.tile([P, 2, P, PACK], F32, name="absx")
+                absx[s // 2] = work.tile([P, 2, P, PACK], F32, name="absx", bufs=3)
             nc.scalar.activation(
                 out=absx[s // 2][:, s % 2], in_=ph[s][:].rearrange("p t n -> p n t"), func=ACT.Abs, bias=shift[:]
             )
 
         def encode_sin(j):
-            ysin[j] = work.tile([P, 2 * P, PACK], F32, name="y")
+            ysin[j] = work.tile([P, 2 * P, PACK], F32, name="y", bufs=4)
             nc.scalar.activation(
                 out=ysin[j][:], in_=absx[j][:].rearrange("p s n t -> p (s n) t"), func=ACT.Sin, bias=hpi[:], scale=-1.0
             )
@@ -150,10 +155,21 @@ def tile_fouriernerffeaturerenderer_kernel(tc, pos, dt, freq, g, w1, ws, w2_byte
         ei, eq, esc = {}, {}, {}
 
         def encode_mul(j):
-            ei[j] = work.tile([P, 2 * P, PACK], BF16, name="ei", align_bytes=64)
+            ei[j] = work.tile([P, 2 * P, PACK], BF16, name="ei", bufs=4, align_bytes=64)
             nc.vector.tensor_tensor(
                 out=ei[j][:], in0=ysin[j][:], in1=g4[:].unsqueeze(1).to_broadcast([P, 2 * P, PACK]), op=ALU.mult
             )
+
+        def encode_mul_g(j):
+            ei[j] = work.tile([P, 2 * P, PACK], BF16, name="ei", bufs=4, align_bytes=64)
+            for q in range(4):
+                n = slice(q * 64, (q + 1) * 64)
+                nc.gpsimd.tensor_tensor(
+                    out=ei[j][:, n, :],
+                    in0=ysin[j][:, n, :],
+                    in1=g4[:].unsqueeze(1).to_broadcast([P, 64, PACK]),
+                    op=ALU.mult,
+                )
 
         def encode_quant(j):
             codes = keep.tile([P, 2 * P], U32, name="eq%d" % j, align_bytes=64)
@@ -196,7 +212,7 @@ def tile_fouriernerffeaturerenderer_kernel(tc, pos, dt, freq, g, w1, ws, w2_byte
 
         def add(s, gi):
             if gi == 0:
-                hi[s] = work.tile([P, G, P, PACK], BF16, name="hi", bufs=2, align_bytes=64)
+                hi[s] = work.tile([P, G, P, PACK], BF16, name="hi", bufs=3, align_bytes=64)
             nc.vector.tensor_tensor(
                 out=hi[s][:, gi], in0=bank_b[s, gi][:].rearrange("p t n -> p n t"), in1=relu_a[s, gi][:], op=ALU.add
             )
@@ -356,17 +372,16 @@ def tile_fouriernerffeaturerenderer_kernel(tc, pos, dt, freq, g, w1, ws, w2_byte
                 nc.sync.dma_start(out=out[:, c * CG : (c + 1) * CG], in_=acc[c][:])
 
         pos_place()
-        pos_turn()
-        pos_copy()
+        for h in range(2):
+            pos_turn(h)
+        for h in range(2):
+            pos_copy(h)
         for s in range(8):
             phase_mm(s)
         def encode_s(j):
             encode_abs(2 * j)
             encode_abs(2 * j + 1)
             encode_sin(j)
-        def encode_v(j):
-            encode_mul(j)
-            encode_quant(j)
         def w2_place(gi):
             for c in range(2):
                 for h in range(2):
@@ -378,63 +393,77 @@ def tile_fouriernerffeaturerenderer_kernel(tc, pos, dt, freq, g, w1, ws, w2_byte
             mm_a(*pairs[i])
             relu(*pairs[i])
         encode_s(0)
+        widen_v(0, 0)
+        widen_v(0, 1)
         w_lay(0, 0, 0)
         w_lay(0, 0, 1)
         w_lay(0, 1, 0)
         w_lay(0, 1, 1)
         w_quant(0, 0)
         encode_s(1)
-        for t in range(4):
-            widen_v(0, t)
-        encode_v(0)
+        widen_v(0, 2)
+        encode_mul(0)
+        w_quant(0, 1)
+        widen_v(0, 3)
+        encode_quant(0)
         encode_s(2)
         w_lay(1, 0, 0)
         w_lay(1, 0, 1)
-        encode_v(1)
-        widen_s(1, 0)
-        w_quant(0, 1)
-        encode_s(3)
-        widen_v(1, 2)
-        widen_v(1, 3)
-        encode_v(2)
-        w2_place(0)
-        widen_s(1, 1)
+        encode_mul(1)
         w_quant(1, 0)
-        gate(0)
-        gate(1)
-        gate(2)
-        gate(3)
+        encode_mul_g(2)
+        encode_s(3)
+        encode_mul_g(3)
         w_lay(1, 1, 0)
         w_lay(1, 1, 1)
-        encode_v(3)
+        encode_quant(1)
+        gate(0)
+        mm_b(*pairs[0])
+        gate(1)
+        w2_place(0)
+        widen_v(1, 2)
         w_quant(1, 1)
-        w2_place(1)
+        widen_v(1, 3)
+        mm_b(*pairs[1])
+        gate(2)
+        gate(3)
+        mm_b(*pairs[2])
+        mm_b(*pairs[3])
+        add(*pairs[0])
         w2_quant(0, 0)
-        w2_quant(0, 1)
+        add(*pairs[1])
+        widen_s(1, 0)
+        widen_s(1, 1)
+        encode_quant(2)
         gate(4)
         gate(5)
-        mm_b(*pairs[0])
-        mm_b(*pairs[1])
-        for i in range(16):
-            if i + 6 < 16:
-                gate(i + 6)
+        for i in range(2, 16):
+            if i + 4 < 16:
+                gate(i + 4)
             if i + 2 < 16:
                 mm_b(*pairs[i + 2])
             add(*pairs[i])
-            if i % 2:
-                h_quant(i // 2)
-            if i in (1, 3):
-                w2_quant(1, i // 2)
-            if i == 7:
+            if i % 2 == 0:
+                h_quant(i // 2 - 1)
+            if i == 3:
+                w2_place(1)
+            if i in (5, 7):
+                w2_quant(1, i // 2 - 2)
+            if i == 2:
+                w2_quant(0, 1)
+            if i == 4:
+                encode_quant(3)
+            if i == 9:
                 u_mm(0)
                 den_a(0)
                 den_b(0)
                 den_c(0)
-            if i == 12:
+            if i == 14:
                 den_d(0)
             if i >= 8:
                 o_mm(*outs[i - 8])
                 sig(*outs[i - 8])
+        h_quant(7)
         u_mm(1)
         for i in range(16):
             if i + 8 < 16:

@@ -83,9 +83,6 @@ def tile_fouriernerffeaturerenderer_kernel(tc, pos, dt, freq, g, w1, ws, w2_byte
         nc.vector.memset(one[:], 1.0)
         hpi = keep.tile([P, 1], F32, name="hpi")
         nc.vector.tensor_scalar(out=hpi[:], in0=one[:, 0:1], scalar1=math.pi / 2, scalar2=None, op0=ALU.mult)
-        base = keep.tile([P, 2, S], F32, name="base")
-        nc.vector.tensor_scalar(out=base[:, 1, :], in0=one[:], scalar1=1.0 / math.e, scalar2=None, op0=ALU.mult)
-        expo = keep.tile([P, 2, S], F32, name="expo")
         trans = keep.tile([P, S + 1], F32, name="trans")
         nc.vector.memset(trans[:, 0:1], 1.0)
         warm = keep.tile([P, 1], F32, name="warm")
@@ -134,10 +131,15 @@ def tile_fouriernerffeaturerenderer_kernel(tc, pos, dt, freq, g, w1, ws, w2_byte
 
         ph, absx, ysin = {}, {}, {}
 
+        frp = keep.tile([P, PACK, P], BF16, name="frp")
+
+        def freq_lay():
+            nc.scalar.copy(out=frp[:], in_=fr[:].rearrange("p (m t) -> p t m", t=PACK))
+
         def phase_mm(s):
             ph[s] = bank([P, PACK, P], F32, "ph")
             for t in range(PACK):
-                nc.tensor.matmul(out=ph[s][:, t, :], lhsT=fr[:, t::PACK], rhs=post[:, s, :], start=True, stop=True)
+                nc.tensor.matmul(out=ph[s][:, t, :], lhsT=frp[:, t, :], rhs=post[:, s, :], start=True, stop=True)
 
         def encode_abs(s):
             if s % 2 == 0:
@@ -159,17 +161,6 @@ def tile_fouriernerffeaturerenderer_kernel(tc, pos, dt, freq, g, w1, ws, w2_byte
             nc.vector.tensor_tensor(
                 out=ei[j][:], in0=ysin[j][:], in1=g4[:].unsqueeze(1).to_broadcast([P, 2 * P, PACK]), op=ALU.mult
             )
-
-        def encode_mul_g(j):
-            ei[j] = work.tile([P, 2 * P, PACK], BF16, name="ei", bufs=4, align_bytes=64)
-            for q in range(4):
-                n = slice(q * 64, (q + 1) * 64)
-                nc.gpsimd.tensor_tensor(
-                    out=ei[j][:, n, :],
-                    in0=ysin[j][:, n, :],
-                    in1=g4[:].unsqueeze(1).to_broadcast([P, 64, PACK]),
-                    op=ALU.mult,
-                )
 
         def encode_quant(j):
             codes = keep.tile([P, 2 * P], U32, name="eq%d" % j, align_bytes=64)
@@ -284,9 +275,12 @@ def tile_fouriernerffeaturerenderer_kernel(tc, pos, dt, freq, g, w1, ws, w2_byte
             )
             w2q[gi, c], w2sc[gi, c] = codes, scales
 
-        absu = keep.tile([P, S], F32, name="absu")
-        powr = keep.tile([P, 2, S], F32, name="powr")
-        quot = keep.tile([P, S], F32, name="quot")
+        arg = keep.tile([P, 2, S], F32, name="arg")
+        sgd = keep.tile([P, 2, S], F32, name="sgd")
+        sgn_z = keep.tile([P, S], F32, name="sgn_z")
+        rec_z = keep.tile([P, S], F32, name="rec_z")
+        pow_u = keep.tile([P, S], F32, name="pow_u")
+        exp_z = keep.tile([P, S], F32, name="exp_z")
         wgt = keep.tile([P, S], F32, name="wgt")
 
         def out_mm(dst, s, gi, c, width):
@@ -313,10 +307,8 @@ def tile_fouriernerffeaturerenderer_kernel(tc, pos, dt, freq, g, w1, ws, w2_byte
             return slice(b * NB, (b + 1) * NB)
 
         def den_a(b):
-            if b == 0:
-                nc.vector.tensor_copy(out=expo[:, 0, :], in_=dtb[:])
             nc.vector.scalar_tensor_tensor(
-                out=expo[:, 1, batch(b)],
+                out=arg[:, 1, batch(b)],
                 in0=u_ps[b][:, :, 0],
                 scalar=0.0,
                 in1=dtb[:, batch(b)],
@@ -325,26 +317,37 @@ def tile_fouriernerffeaturerenderer_kernel(tc, pos, dt, freq, g, w1, ws, w2_byte
             )
 
         def den_b(b):
-            nc.scalar.activation(out=absu[:, batch(b)], in_=u_ps[b][:, :, 0], func=ACT.Abs)
-            nc.scalar.activation(out=base[:, 0, batch(b)], in_=absu[:, batch(b)], func=ACT.Sigmoid)
+            q = batch(b)
+            nc.scalar.activation(out=arg[:, 0, q], in_=u_ps[b][:, :, 0], func=ACT.Abs)
+            nc.scalar.activation(out=sgn_z[:, q], in_=arg[:, 1, q], func=ACT.Sigmoid, scale=-1.0)
+            nc.scalar.activation(out=sgd[:, :, q], in_=arg[:, :, q], func=ACT.Sigmoid)
 
         def den_c(b):
             q = batch(b)
-            nc.gpsimd.tensor_tensor(out=powr[:, :, q], in0=base[:, :, q], in1=expo[:, :, q], op=ALU.pow)
-            nc.gpsimd.tensor_tensor(out=quot[:, q], in0=powr[:, 0, q], in1=powr[:, 1, q], op=ALU.mult)
+            nc.gpsimd.tensor_tensor(out=pow_u[:, q], in0=sgd[:, 0, q], in1=dtb[:, q], op=ALU.pow)
+
+        def den_r(b):
+            q = batch(b)
+            nc.vector.reciprocal(out=rec_z[:, q], in_=sgd[:, 1, q])
+            nc.gpsimd.tensor_tensor(out=exp_z[:, q], in0=sgn_z[:, q], in1=rec_z[:, q], op=ALU.mult)
 
         def den_d(b):
-            q = batch(b)
-            nxt = slice(b * NB + 1, (b + 1) * NB + 1)
             nc.vector.tensor_tensor_scan(
-                out=trans[:, nxt],
-                data0=quot[:, q],
-                data1=one[:, q],
+                out=trans[:, b * NB + 1 : (b + 1) * NB + 1],
+                data0=pow_u[:, batch(b)],
+                data1=exp_z[:, batch(b)],
                 initial=trans[:, b * NB : b * NB + 1],
                 op0=ALU.mult,
                 op1=ALU.mult,
             )
-            nc.vector.tensor_tensor(out=wgt[:, q], in0=trans[:, q], in1=trans[:, nxt], op=ALU.subtract)
+
+        def den_w(b):
+            nc.vector.tensor_tensor(
+                out=wgt[:, batch(b)],
+                in0=trans[:, batch(b)],
+                in1=trans[:, b * NB + 1 : (b + 1) * NB + 1],
+                op=ALU.subtract,
+            )
 
         def o_mm(s, c):
             o_ps[s, c] = bank([P, CG], F32, "o_ps")
@@ -372,6 +375,7 @@ def tile_fouriernerffeaturerenderer_kernel(tc, pos, dt, freq, g, w1, ws, w2_byte
                 nc.sync.dma_start(out=out[:, c * CG : (c + 1) * CG], in_=acc[c][:])
 
         pos_place()
+        freq_lay()
         for h in range(2):
             pos_turn(h)
         for h in range(2):
@@ -398,81 +402,85 @@ def tile_fouriernerffeaturerenderer_kernel(tc, pos, dt, freq, g, w1, ws, w2_byte
         w_lay(0, 0, 0)
         w_lay(0, 0, 1)
         w_lay(0, 1, 0)
-        w_lay(0, 1, 1)
-        w_quant(0, 0)
-        encode_s(1)
         widen_v(0, 2)
-        encode_mul(0)
-        w_quant(0, 1)
+        w_quant(0, 0)
         widen_v(0, 3)
+        encode_s(1)
+        encode_mul(0)
+        w_lay(0, 1, 1)
         encode_quant(0)
+        widen_v(1, 0)
+        w_quant(0, 1)
         encode_s(2)
+        w2_place(0)
+        encode_mul(1)
+        widen_v(1, 1)
+        encode_quant(1)
+        widen_v(1, 2)
+        widen_v(1, 3)
+        encode_s(3)
         w_lay(1, 0, 0)
         w_lay(1, 0, 1)
-        encode_mul(1)
+        encode_mul(2)
         w_quant(1, 0)
-        encode_mul_g(2)
-        encode_s(3)
-        encode_mul_g(3)
+        encode_quant(2)
+        gate(0)
+        gate(1)
+        mm_b(*pairs[0])
+        w2_place(1)
         w_lay(1, 1, 0)
         w_lay(1, 1, 1)
-        encode_quant(1)
-        gate(0)
-        mm_b(*pairs[0])
-        gate(1)
-        w2_place(0)
-        widen_v(1, 2)
+        encode_mul(3)
         w_quant(1, 1)
-        widen_v(1, 3)
-        mm_b(*pairs[1])
+        encode_quant(3)
         gate(2)
         gate(3)
-        mm_b(*pairs[2])
-        mm_b(*pairs[3])
-        add(*pairs[0])
+        mm_b(*pairs[1])
         w2_quant(0, 0)
-        add(*pairs[1])
-        widen_s(1, 0)
-        widen_s(1, 1)
-        encode_quant(2)
+        w2_quant(0, 1)
         gate(4)
+        mm_b(*pairs[2])
         gate(5)
-        for i in range(2, 16):
-            if i + 4 < 16:
-                gate(i + 4)
-            if i + 2 < 16:
+        mm_b(*pairs[3])
+        for i in range(16):
+            if i + 6 < 16:
+                gate(i + 6)
+            if 4 <= i + 2 < 16:
                 mm_b(*pairs[i + 2])
             add(*pairs[i])
-            if i % 2 == 0:
+            if i % 2 == 0 and i:
                 h_quant(i // 2 - 1)
-            if i == 3:
-                w2_place(1)
-            if i in (5, 7):
-                w2_quant(1, i // 2 - 2)
-            if i == 2:
-                w2_quant(0, 1)
-            if i == 4:
-                encode_quant(3)
-            if i == 9:
+            if i in (1, 3):
+                w2_quant(1, i // 2)
+            if i == 8:
                 u_mm(0)
+            if i == 9:
                 den_a(0)
                 den_b(0)
                 den_c(0)
+            if i == 12:
+                den_r(0)
             if i == 14:
                 den_d(0)
-            if i >= 8:
-                o_mm(*outs[i - 8])
-                sig(*outs[i - 8])
+            if i == 15:
+                den_w(0)
+            if i >= 6:
+                o_mm(*outs[i - 6])
+                sig(*outs[i - 6])
         h_quant(7)
         u_mm(1)
         for i in range(16):
-            if i + 8 < 16:
-                o_mm(*outs[i + 8])
-                sig(*outs[i + 8])
             comp(*outs[i])
             if i == 1:
                 den_a(1)
                 den_b(1)
                 den_c(1)
-            if i == 7:
+            if i + 10 < 16:
+                o_mm(*outs[i + 10])
+                sig(*outs[i + 10])
+            if i == 4:
+                den_r(1)
+            if i == 6:
                 den_d(1)
+            if i == 7:
+                den_w(1)

@@ -62,14 +62,13 @@ def tile_fouriernerffeaturerenderer_kernel(tc, pos, dt, freq, g, w1, ws, w2_byte
         def load_w2(gi, t0, t1):
             nc.sync.dma_start(out=w2b[gi][:, t0:t1, :], in_=w2_view[gi][:, t0:t1, :])
 
-        load_w2(0, 0, 2)
         load_w(0, 0, 0, CG // 2)
         load_w(0, 0, CG // 2, CG)
         load_w(0, 1, 0, CG)
-        load_w2(0, 2, 4)
+        load_w2(0, 0, 4)
+        load_w2(1, 0, 4)
         load_w(1, 0, 0, CG)
         load_w(1, 1, 0, CG)
-        load_w2(1, 0, 4)
 
         ident = keep.tile([P, P], BF16, name="ident")
         make_identity(nc, ident[:])
@@ -110,17 +109,8 @@ def tile_fouriernerffeaturerenderer_kernel(tc, pos, dt, freq, g, w1, ws, w2_byte
                 wi[gi, br] = work.tile([P, CG * PACK], BF16, name="wi", bufs=3, align_bytes=64)
             m = slice(h * 64, (h + 1) * 64)
             nc.vector.tensor_copy(
-                out=wi[gi, br][:].rearrange("p (t m j) -> p t m j", t=PACK, j=PACK)[:, :, m, :],
-                in_=raw[gi, br][:].rearrange("p j (m t) -> p t m j", t=PACK)[:, :, m, :],
-            )
-
-        def w_lay_s(gi, br, h):
-            if h == 0:
-                wi[gi, br] = work.tile([P, CG * PACK], BF16, name="wi", bufs=3, align_bytes=64)
-            m = slice(h * 64, (h + 1) * 64)
-            nc.scalar.copy(
-                out=wi[gi, br][:].rearrange("p (t m j) -> p t m j", t=PACK, j=PACK)[:, :, m, :],
-                in_=raw[gi, br][:].rearrange("p j (m t) -> p t m j", t=PACK)[:, :, m, :],
+                out=wi[gi, br][:].rearrange("p (t m j) -> p m t j", t=PACK, j=PACK)[:, m],
+                in_=raw[gi, br][:].rearrange("p j (m t) -> p m t j", t=PACK)[:, m],
             )
 
         def w_quant(gi, br):
@@ -386,72 +376,78 @@ def tile_fouriernerffeaturerenderer_kernel(tc, pos, dt, freq, g, w1, ws, w2_byte
             encode_abs(2 * j)
             encode_abs(2 * j + 1)
             encode_sin(j)
-        def w2_place(gi):
-            for c in range(2):
-                for h in range(2):
-                    lay(gi, c, h)
-                    lay_copy(gi, c, h)
+        blocks = [(gi, c, h) for gi in range(2) for c in range(2) for h in range(2)]
         pairs = [(s, gi) for s in range(8) for gi in range(2)]
+        gates = [(0, 0), (1, 0), (0, 1), (1, 1)] + pairs[4:]
         outs = [(s, c) for s in range(8) for c in range(2)]
         def gate(i):
-            mm_a(*pairs[i])
-            relu(*pairs[i])
+            mm_a(*gates[i])
+            relu(*gates[i])
         encode_s(0)
-        widen_v(0, 0)
-        widen_v(0, 1)
         w_lay(0, 0, 0)
         w_lay(0, 0, 1)
         w_lay(0, 1, 0)
-        widen_v(0, 2)
+        w_lay(0, 1, 1)
         w_quant(0, 0)
-        widen_v(0, 3)
+        widen_v(0, 0)
+        w_quant(0, 1)
+        widen_v(0, 1)
         encode_s(1)
         encode_mul(0)
-        w_lay(0, 1, 1)
+        widen_v(0, 2)
         encode_quant(0)
-        widen_v(1, 0)
-        w_quant(0, 1)
+        widen_v(0, 3)
         encode_s(2)
-        w2_place(0)
-        encode_mul(1)
-        widen_v(1, 1)
-        encode_quant(1)
-        widen_v(1, 2)
-        widen_v(1, 3)
-        encode_s(3)
         w_lay(1, 0, 0)
+        encode_mul(1)
         w_lay(1, 0, 1)
-        encode_mul(2)
-        w_quant(1, 0)
-        encode_quant(2)
         gate(0)
+        encode_quant(1)
+        lay(*blocks[0])
+        widen_v(1, 0)
+        encode_s(3)
+        w_quant(1, 0)
         gate(1)
-        mm_b(*pairs[0])
-        w2_place(1)
+        lay(*blocks[1])
+        widen_v(1, 1)
+        widen_s(1, 2)
+        lay_copy(*blocks[0])
+        lay(*blocks[2])
+        widen_s(1, 3)
+        lay_copy(*blocks[1])
+        encode_mul(2)
+        gate(2)
+        lay(*blocks[3])
         w_lay(1, 1, 0)
+        encode_quant(2)
+        lay_copy(*blocks[2])
+        gate(3)
         w_lay(1, 1, 1)
+        mm_b(*pairs[0])
+        lay_copy(*blocks[3])
+        gate(4)
+        lay(*blocks[4])
         encode_mul(3)
         w_quant(1, 1)
         encode_quant(3)
-        gate(2)
-        gate(3)
         mm_b(*pairs[1])
-        w2_quant(0, 0)
-        w2_quant(0, 1)
-        gate(4)
-        mm_b(*pairs[2])
         gate(5)
+        mm_b(*pairs[2])
         mm_b(*pairs[3])
         for i in range(16):
             if i + 6 < 16:
                 gate(i + 6)
+            if i < 4:
+                lay_copy(*blocks[i + 4])
+                if i < 3:
+                    lay(*blocks[i + 5])
             if 4 <= i + 2 < 16:
                 mm_b(*pairs[i + 2])
             add(*pairs[i])
             if i % 2 == 0 and i:
                 h_quant(i // 2 - 1)
-            if i in (1, 3):
-                w2_quant(1, i // 2)
+            if i in (1, 3, 4, 6):
+                w2_quant(*((0, 0), (0, 1), (1, 0), (1, 1))[(1, 3, 4, 6).index(i)])
             if i == 8:
                 u_mm(0)
             if i == 9:
@@ -464,9 +460,9 @@ def tile_fouriernerffeaturerenderer_kernel(tc, pos, dt, freq, g, w1, ws, w2_byte
                 den_d(0)
             if i == 15:
                 den_w(0)
-            if i >= 6:
-                o_mm(*outs[i - 6])
-                sig(*outs[i - 6])
+            if i >= 7:
+                o_mm(*outs[i - 7])
+                sig(*outs[i - 7])
         h_quant(7)
         u_mm(1)
         for i in range(16):
@@ -475,9 +471,9 @@ def tile_fouriernerffeaturerenderer_kernel(tc, pos, dt, freq, g, w1, ws, w2_byte
                 den_a(1)
                 den_b(1)
                 den_c(1)
-            if i + 10 < 16:
-                o_mm(*outs[i + 10])
-                sig(*outs[i + 10])
+            if i + 9 < 16:
+                o_mm(*outs[i + 9])
+                sig(*outs[i + 9])
             if i == 4:
                 den_r(1)
             if i == 6:

@@ -100,17 +100,16 @@ def tile_fouriernerffeaturerenderer_kernel(tc, pos, dt, freq, g, w1, ws, w2_byte
             state[h] = t
 
         def pos_copy(h):
-            nc.scalar.copy(out=post[:, h * (S // 2) : (h + 1) * (S // 2), :], in_=state[h][:])
+            nc.scalar.copy(out=post[:, h * (S // 2) : (h + 1) * (S // 2), :].bitcast(F32), in_=state[h][:].bitcast(F32))
 
         wi, wq, wsc = {}, {}, {}
 
-        def w_lay(gi, br, h):
-            if h == 0:
+        def w_lay(gi, br, m0, m1):
+            if m0 == 0:
                 wi[gi, br] = work.tile([P, CG * PACK], BF16, name="wi", bufs=3, align_bytes=64)
-            m = slice(h * 64, (h + 1) * 64)
             nc.vector.tensor_copy(
-                out=wi[gi, br][:].rearrange("p (t m j) -> p m t j", t=PACK, j=PACK)[:, m],
-                in_=raw[gi, br][:].rearrange("p j (m t) -> p m t j", t=PACK)[:, m],
+                out=wi[gi, br][:].rearrange("p (t m j) -> p m t j", t=PACK, j=PACK)[:, m0:m1],
+                in_=raw[gi, br][:].rearrange("p j (m t) -> p m t j", t=PACK)[:, m0:m1],
             )
 
         def w_quant(gi, br):
@@ -244,7 +243,7 @@ def tile_fouriernerffeaturerenderer_kernel(tc, pos, dt, freq, g, w1, ws, w2_byte
         def lay_copy(gi, c, h):
             if h == 0:
                 w2i[gi, c] = work.tile([P, CG, PACK], BF16, name="w2i", bufs=4, align_bytes=64)
-            nc.scalar.copy(out=w2i[gi, c][:, h * 2 * P : (h + 1) * 2 * P, :], in_=w2ps[gi, c, h][:])
+            nc.scalar.copy(out=w2i[gi, c][:, h * 2 * P : (h + 1) * 2 * P, :].bitcast(F32), in_=w2ps[gi, c, h][:].bitcast(F32))
 
         def lay_copy_v(gi, c, h):
             if h == 0:
@@ -350,19 +349,24 @@ def tile_fouriernerffeaturerenderer_kernel(tc, pos, dt, freq, g, w1, ws, w2_byte
 
         acc = {}
 
-        def comp(s, c):
-            t = work.tile([P, CG], F32, name="acc%d" % c)
+        def comp(s, c, c0, c1):
+            if c0 == 0:
+                acc[s, c] = work.tile([P, CG], F32, name="acc%d" % c, bufs=3)
             if s == 0:
                 nc.vector.tensor_scalar(
-                    out=t[:], in0=sgm[s, c][:], scalar1=wgt[:, s : s + 1], scalar2=None, op0=ALU.mult
+                    out=acc[s, c][:, c0:c1], in0=sgm[s, c][:, c0:c1], scalar1=wgt[:, s : s + 1], scalar2=None, op0=ALU.mult
                 )
             else:
                 nc.vector.scalar_tensor_tensor(
-                    out=t[:], in0=sgm[s, c][:], scalar=wgt[:, s : s + 1], in1=acc[c][:], op0=ALU.mult, op1=ALU.add
+                    out=acc[s, c][:, c0:c1],
+                    in0=sgm[s, c][:, c0:c1],
+                    scalar=wgt[:, s : s + 1],
+                    in1=acc[s - 1, c][:, c0:c1],
+                    op0=ALU.mult,
+                    op1=ALU.add,
                 )
-            acc[c] = t
             if s == S - 1:
-                nc.sync.dma_start(out=out[:, c * CG : (c + 1) * CG], in_=acc[c][:])
+                nc.sync.dma_start(out=out[:, c * CG + c0 : c * CG + c1], in_=acc[s, c][:, c0:c1])
 
         pos_place()
         freq_lay()
@@ -379,15 +383,16 @@ def tile_fouriernerffeaturerenderer_kernel(tc, pos, dt, freq, g, w1, ws, w2_byte
         blocks = [(gi, c, h) for gi in range(2) for c in range(2) for h in range(2)]
         pairs = [(s, gi) for s in range(8) for gi in range(2)]
         gates = [(0, 0), (1, 0), (0, 1), (1, 1)] + pairs[4:]
-        outs = [(s, c) for s in range(8) for c in range(2)]
+        outs = pairs
+        comps = [(s, c, 0, CG) for s in range(6) for c in range(2)]
+        comps += [(6, 0, 0, CG), (6, 1, 0, CG // 2), (7, 0, 0, CG), (6, 1, CG // 2, CG), (7, 1, 0, CG // 2), (7, 1, CG // 2, CG)]
         def gate(i):
             mm_a(*gates[i])
             relu(*gates[i])
         encode_s(0)
-        w_lay(0, 0, 0)
-        w_lay(0, 0, 1)
-        w_lay(0, 1, 0)
-        w_lay(0, 1, 1)
+        w_lay(0, 0, 0, 64)
+        w_lay(0, 0, 64, 128)
+        w_lay(0, 1, 0, 128)
         w_quant(0, 0)
         widen_v(0, 0)
         w_quant(0, 1)
@@ -398,9 +403,8 @@ def tile_fouriernerffeaturerenderer_kernel(tc, pos, dt, freq, g, w1, ws, w2_byte
         encode_quant(0)
         widen_v(0, 3)
         encode_s(2)
-        w_lay(1, 0, 0)
         encode_mul(1)
-        w_lay(1, 0, 1)
+        w_lay(1, 0, 0, 128)
         gate(0)
         encode_quant(1)
         lay(*blocks[0])
@@ -418,31 +422,32 @@ def tile_fouriernerffeaturerenderer_kernel(tc, pos, dt, freq, g, w1, ws, w2_byte
         encode_mul(2)
         gate(2)
         lay(*blocks[3])
-        w_lay(1, 1, 0)
+        w_lay(1, 1, 0, 128)
         encode_quant(2)
         lay_copy(*blocks[2])
         gate(3)
-        w_lay(1, 1, 1)
         mm_b(*pairs[0])
+        mm_b(*pairs[2])
         lay_copy(*blocks[3])
         gate(4)
         lay(*blocks[4])
         encode_mul(3)
         w_quant(1, 1)
         encode_quant(3)
-        mm_b(*pairs[1])
         gate(5)
-        mm_b(*pairs[2])
+        lay(*blocks[5])
+        lay_copy(*blocks[4])
+        mm_b(*pairs[1])
         mm_b(*pairs[3])
         for i in range(16):
             if i + 6 < 16:
                 gate(i + 6)
-            if i < 4:
-                lay_copy(*blocks[i + 4])
-                if i < 3:
-                    lay(*blocks[i + 5])
-            if 4 <= i + 2 < 16:
-                mm_b(*pairs[i + 2])
+            if i < 3:
+                lay_copy(*blocks[i + 5])
+            if i + 4 < 16:
+                mm_b(*pairs[i + 4])
+            if i < 2:
+                lay(*blocks[i + 6])
             add(*pairs[i])
             if i % 2 == 0 and i:
                 h_quant(i // 2 - 1)
@@ -450,30 +455,29 @@ def tile_fouriernerffeaturerenderer_kernel(tc, pos, dt, freq, g, w1, ws, w2_byte
                 w2_quant(*((0, 0), (0, 1), (1, 0), (1, 1))[(1, 3, 4, 6).index(i)])
             if i == 8:
                 u_mm(0)
-            if i == 9:
+            if i == 10:
                 den_a(0)
                 den_b(0)
                 den_c(0)
-            if i == 12:
+            if i == 13:
                 den_r(0)
-            if i == 14:
-                den_d(0)
             if i == 15:
-                den_w(0)
-            if i >= 7:
-                o_mm(*outs[i - 7])
-                sig(*outs[i - 7])
+                den_d(0)
+            if i >= 10:
+                o_mm(*outs[i - 10])
+                sig(*outs[i - 10])
         h_quant(7)
+        den_w(0)
         u_mm(1)
-        for i in range(16):
-            comp(*outs[i])
+        for i, piece in enumerate(comps):
+            comp(*piece)
             if i == 1:
                 den_a(1)
                 den_b(1)
                 den_c(1)
-            if i + 9 < 16:
-                o_mm(*outs[i + 9])
-                sig(*outs[i + 9])
+            if i + 6 < 16:
+                o_mm(*outs[i + 6])
+                sig(*outs[i + 6])
             if i == 4:
                 den_r(1)
             if i == 6:

import math
from contextlib import ExitStack

import concourse.mybir as mybir
from concourse.masks import make_identity

R, S, F, F2, C = 128, 8, 256, 512, 1024
P = 128
PACK = 4
G = 2
CG = 512
NB = 4
FLOPS = 2 * R * S * (2 * F2 * C + C * C)

F32 = mybir.dt.float32
BF16 = mybir.dt.bfloat16
U32 = mybir.dt.uint32
U8 = mybir.dt.uint8
FP8 = mybir.dt.float8_e4m3fn
FP8X4 = mybir.dt.float8_e4m3fn_x4
ACT = mybir.ActivationFunctionType
ALU = mybir.AluOpType


def tile_fouriernerffeaturerenderer_kernel(tc, pos, dt, freq, g, w1, ws, w2_bytes, w2_scale, out):
    nc = tc.nc
    with ExitStack() as ctx:
        keep = ctx.enter_context(tc.tile_pool(name="keep", bufs=1))
        work = ctx.enter_context(tc.tile_pool(name="work", bufs=2))
        psum = ctx.enter_context(tc.psum_pool(name="psum", bufs=8))
        ctx.enter_context(tc.manual_schedule())

        def bank(shape, dtype, name):
            return psum.tile(shape, dtype, name=name, tag="bank", bufs=8)

        fr = keep.tile([P, F2], BF16, name="fr")
        nc.vector.memset(fr[:], 0.0)
        pb = keep.tile([P, S, P], BF16, name="pb")
        nc.gpsimd.memset(pb[:], 0.0)
        posr = keep.tile([P, S, 3], BF16, name="posr")
        nc.sync.dma_start(out=posr[:], in_=pos)
        for h in range(2):
            nc.scalar.dma_start(out=fr[0:3, h * F : (h + 1) * F], in_=freq)
        g4 = keep.tile([P, PACK], BF16, name="g4")
        nc.scalar.dma_start(out=g4[:], in_=g.rearrange("(p t) -> p t", t=PACK))
        w2s = keep.tile([P, G, PACK], F32, name="w2s")
        nc.scalar.dma_start(out=w2s[:], in_=w2_scale.rearrange("(g p t) o -> p g (t o)", p=P, t=PACK))
        dtb = keep.tile([P, S], BF16, name="dtb")
        nc.scalar.dma_start(out=dtb[:], in_=dt)

        raw, w2b = {}, {}
        for gi in range(G):
            for br in range(2):
                raw[gi, br] = keep.tile([P, PACK, CG], BF16, name="raw%d%d" % (gi, br))
            w2b[gi] = keep.tile([P, PACK, C], U8, name="w2b%d" % gi)
        w2_view = w2_bytes.rearrange("(g p t) n -> g p t n", p=P, t=PACK)
        w_view = [src.rearrange("(p j) c -> p j c", j=PACK) for src in (w1, ws)]

        def load_w(gi, br, c0, c1):
            nc.sync.dma_start(out=raw[gi, br][:, :, c0:c1], in_=w_view[br][:, :, gi * CG + c0 : gi * CG + c1])

        def load_w2(gi, t0, t1):
            nc.sync.dma_start(out=w2b[gi][:, t0:t1, :], in_=w2_view[gi][:, t0:t1, :])

        load_w(0, 0, 0, CG // 2)
        load_w(0, 0, CG // 2, CG)
        load_w(0, 1, 0, CG)
        load_w2(0, 0, 4)
        load_w2(1, 0, 4)
        load_w(1, 0, 0, CG)
        load_w(1, 1, 0, CG)

        ident = keep.tile([P, P], BF16, name="ident")
        make_identity(nc, ident[:])

        sgn = keep.tile([P, 1], F32, name="sgn")
        nc.vector.memset(sgn[0:64], -1.0)
        nc.vector.memset(sgn[64:128], 0.0)
        shift = keep.tile([P, 1], F32, name="shift")
        nc.vector.tensor_scalar(out=shift[:], in0=sgn[:], scalar1=math.pi / 2, scalar2=None, op0=ALU.mult)
        one = keep.tile([P, S], F32, name="one")
        nc.vector.memset(one[:], 1.0)
        hpi = keep.tile([P, 1], F32, name="hpi")
        nc.vector.tensor_scalar(out=hpi[:], in0=one[:, 0:1], scalar1=math.pi / 2, scalar2=None, op0=ALU.mult)
        trans = keep.tile([P, S + 1], F32, name="trans")
        nc.vector.memset(trans[:, 0:1], 1.0)
        warm = keep.tile([P, 1], F32, name="warm")
        nc.scalar.activation(out=warm[:], in_=sgn[:], func=ACT.Sin)

        post = keep.tile([P, S, P], BF16, name="post")
        state = {}

        def pos_place():
            nc.vector.tensor_copy(out=pb[:, :, 0:3], in_=posr[:])

        def pos_turn(h):
            t = bank([P, S // 2, P], BF16, "pos_ps")
            for s in range(S // 2):
                nc.tensor.transpose(t[:, s, :], pb[:, h * (S // 2) + s, :], ident[:])
            state[h] = t

        def pos_copy(h):
            nc.scalar.copy(out=post[:, h * (S // 2) : (h + 1) * (S // 2), :].bitcast(F32), in_=state[h][:].bitcast(F32))

        wi, wq, wsc = {}, {}, {}

        def w_lay(gi, br, m0, m1):
            if m0 == 0:
                wi[gi, br] = work.tile([P, CG * PACK], BF16, name="wi", bufs=3, align_bytes=64)
            nc.vector.tensor_copy(
                out=wi[gi, br][:].rearrange("p (t m j) -> p m t j", t=PACK, j=PACK)[:, m0:m1],
                in_=raw[gi, br][:].rearrange("p j (m t) -> p m t j", t=PACK)[:, m0:m1],
            )

        def w_quant(gi, br):
            codes = keep.tile([P, CG], U32, name="wq%d%d" % (gi, br), align_bytes=64)
            scales = keep.tile([P, CG], U8, name="wsc%d%d" % (gi, br), align_bytes=64)
            nc.vector.quantize_mx(out=codes[:].bitcast(FP8X4), scales=scales[:], in_=wi[gi, br][:])
            wq[gi, br], wsc[gi, br] = codes, scales

        ph, absx, ysin = {}, {}, {}

        frp = keep.tile([P, PACK, P], BF16, name="frp")

        def freq_lay():
            nc.scalar.copy(out=frp[:], in_=fr[:].rearrange("p (m t) -> p t m", t=PACK))

        def phase_mm(s):
            ph[s] = bank([P, PACK, P], F32, "ph")
            for t in range(PACK):
                nc.tensor.matmul(out=ph[s][:, t, :], lhsT=frp[:, t, :], rhs=post[:, s, :], start=True, stop=True)

        def encode_abs(s):
            if s % 2 == 0:
                absx[s // 2] = work.tile([P, 2, P, PACK], F32, name="absx", bufs=3)
            nc.scalar.activation(
                out=absx[s // 2][:, s % 2], in_=ph[s][:].rearrange("p t n -> p n t"), func=ACT.Abs, bias=shift[:]
            )

        def encode_sin(j):
            ysin[j] = work.tile([P, 2 * P, PACK], F32, name="y", bufs=4)
            nc.scalar.activation(
                out=ysin[j][:], in_=absx[j][:].rearrange("p s n t -> p (s n) t"), func=ACT.Sin, bias=hpi[:], scale=-1.0
            )

        ei, eq, esc = {}, {}, {}

        def encode_mul(j):
            ei[j] = work.tile([P, 2 * P, PACK], BF16, name="ei", bufs=4, align_bytes=64)
            nc.vector.tensor_tensor(
                out=ei[j][:], in0=ysin[j][:], in1=g4[:].unsqueeze(1).to_broadcast([P, 2 * P, PACK]), op=ALU.mult
            )

        def encode_quant(j):
            codes = keep.tile([P, 2 * P], U32, name="eq%d" % j, align_bytes=64)
            scales = keep.tile([P, 2 * P], U8, name="esc%d" % j, align_bytes=64)
            nc.vector.quantize_mx(
                out=codes[:].bitcast(FP8X4), scales=scales[:], in_=ei[j][:].rearrange("p n t -> p (n t)")
            )
            eq[j], esc[j] = codes, scales

        hi, hq, hsc = {}, {}, {}
        bank_a, bank_b, relu_a = {}, {}, {}

        def hidden_mm(s, gi, br, name):
            cols = slice((s % 2) * P, (s % 2 + 1) * P)
            t_bank = bank([P, PACK, P], F32, name)
            for t in range(PACK):
                m = slice(t * P, (t + 1) * P)
                nc.tensor.matmul_mx(
                    out=t_bank[:, t, :],
                    lhsT=wq[gi, br][:, m].bitcast(FP8X4),
                    lhsT_scale=wsc[gi, br][:, m],
                    rhs=eq[s // 2][:, cols].bitcast(FP8X4),
                    rhs_scale=esc[s // 2][:, cols],
                    start=True,
                    stop=True,
                )
            return t_bank

        def mm_a(s, gi):
            bank_a[s, gi] = hidden_mm(s, gi, 0, "ba")

        def mm_b(s, gi):
            bank_b[s, gi] = hidden_mm(s, gi, 1, "bb")

        def relu(s, gi):
            relu_a[s, gi] = work.tile([P, P, PACK], F32, name="relu", bufs=8)
            nc.scalar.activation(
                out=relu_a[s, gi][:], in_=bank_a[s, gi][:].rearrange("p t n -> p n t"), func=ACT.Relu
            )

        def add(s, gi):
            if gi == 0:
                hi[s] = work.tile([P, G, P, PACK], BF16, name="hi", bufs=3, align_bytes=64)
            nc.vector.tensor_tensor(
                out=hi[s][:, gi], in0=bank_b[s, gi][:].rearrange("p t n -> p n t"), in1=relu_a[s, gi][:], op=ALU.add
            )

        def h_quant(s):
            codes = keep.tile([P, G * P], U32, name="hq%d" % s, align_bytes=64)
            scales = keep.tile([P, G * P], U8, name="hsc%d" % s, align_bytes=64)
            nc.vector.quantize_mx(
                out=codes[:].bitcast(FP8X4), scales=scales[:], in_=hi[s][:].rearrange("p g n t -> p (g n t)")
            )
            hq[s], hsc[s] = codes, scales

        w2w, w2i, w2ps = {}, {}, {}
        w2q, w2sc = {}, {}

        def w2_wide(gi):
            if gi not in w2w:
                w2w[gi] = keep.tile([P, PACK, C], BF16, name="w2w%d" % gi)
            return w2w[gi]

        def widen_s(gi, t):
            nc.scalar.activation(
                out=w2_wide(gi)[:, t, :], in_=w2b[gi][:, t, :].bitcast(FP8), func=ACT.Copy, scale=w2s[:, gi, t : t + 1]
            )

        def widen_v(gi, t):
            nc.vector.tensor_scalar(
                out=w2_wide(gi)[:, t, :],
                in0=w2b[gi][:, t, :].bitcast(FP8),
                scalar1=w2s[:, gi, t : t + 1],
                scalar2=None,
                op0=ALU.mult,
            )

        def lay(gi, c, h):
            t_bank = bank([P, 2 * P, PACK], BF16, "lay")
            for q in range(2):
                n0 = c * CG + h * 2 * P + q * P
                nc.tensor.matmul(
                    out=t_bank[:, q * P : (q + 1) * P, :],
                    lhsT=ident[:],
                    rhs=w2w[gi][:, :, n0 : n0 + P].rearrange("p t c -> p c t"),
                    start=True,
                    stop=True,
                )
            w2ps[gi, c, h] = t_bank

        def lay_copy(gi, c, h):
            if h == 0:
                w2i[gi, c] = work.tile([P, CG, PACK], BF16, name="w2i", bufs=4, align_bytes=64)
            nc.scalar.copy(out=w2i[gi, c][:, h * 2 * P : (h + 1) * 2 * P, :].bitcast(F32), in_=w2ps[gi, c, h][:].bitcast(F32))

        def lay_copy_v(gi, c, h):
            if h == 0:
                w2i[gi, c] = work.tile([P, CG, PACK], BF16, name="w2i", bufs=4, align_bytes=64)
            nc.vector.tensor_copy(out=w2i[gi, c][:, h * 2 * P : (h + 1) * 2 * P, :], in_=w2ps[gi, c, h][:])

        def lay_direct(gi, c):
            w2i[gi, c] = work.tile([P, CG, PACK], BF16, name="w2i", bufs=4, align_bytes=64)
            nc.vector.tensor_copy(
                out=w2i[gi, c][:], in_=w2w[gi][:, :, c * CG : (c + 1) * CG].rearrange("p t c -> p c t")
            )

        def w2_quant(gi, c):
            codes = keep.tile([P, CG], U32, name="w2q%d%d" % (gi, c), align_bytes=64)
            scales = keep.tile([P, CG], U8, name="w2sc%d%d" % (gi, c), align_bytes=64)
            nc.vector.quantize_mx(
                out=codes[:].bitcast(FP8X4), scales=scales[:], in_=w2i[gi, c][:].rearrange("p c t -> p (c t)")
            )
            w2q[gi, c], w2sc[gi, c] = codes, scales

        arg = keep.tile([P, 2, S], F32, name="arg")
        sgd = keep.tile([P, 2, S], F32, name="sgd")
        sgn_z = keep.tile([P, S], F32, name="sgn_z")
        rec_z = keep.tile([P, S], F32, name="rec_z")
        pow_u = keep.tile([P, S], F32, name="pow_u")
        exp_z = keep.tile([P, S], F32, name="exp_z")
        wgt = keep.tile([P, S], F32, name="wgt")

        def out_mm(dst, s, gi, c, width):
            m = slice(gi * P, (gi + 1) * P)
            nc.tensor.matmul_mx(
                out=dst,
                lhsT=hq[s][:, m].bitcast(FP8X4),
                lhsT_scale=hsc[s][:, m],
                rhs=w2q[gi, c][:, 0:width].bitcast(FP8X4),
                rhs_scale=w2sc[gi, c][:, 0:width],
                start=(gi == 0),
                stop=(gi == G - 1),
            )

        u_ps, o_ps, sgm = {}, {}, {}

        def u_mm(b):
            u_ps[b] = bank([P, NB, P], F32, "u_ps")
            for k in range(NB):
                for gi in range(G):
                    out_mm(u_ps[b][:, k, :], b * NB + k, gi, 0, P)

        def batch(b):
            return slice(b * NB, (b + 1) * NB)

        def den_a(b):
            nc.vector.scalar_tensor_tensor(
                out=arg[:, 1, batch(b)],
                in0=u_ps[b][:, :, 0],
                scalar=0.0,
                in1=dtb[:, batch(b)],
                op0=ALU.max,
                op1=ALU.mult,
            )

        def den_b(b):
            q = batch(b)
            nc.scalar.activation(out=arg[:, 0, q], in_=u_ps[b][:, :, 0], func=ACT.Abs)
            nc.scalar.activation(out=sgn_z[:, q], in_=arg[:, 1, q], func=ACT.Sigmoid, scale=-1.0)
            nc.scalar.activation(out=sgd[:, :, q], in_=arg[:, :, q], func=ACT.Sigmoid)

        def den_c(b):
            q = batch(b)
            nc.gpsimd.tensor_tensor(out=pow_u[:, q], in0=sgd[:, 0, q], in1=dtb[:, q], op=ALU.pow)

        def den_r(b):
            q = batch(b)
            nc.vector.reciprocal(out=rec_z[:, q], in_=sgd[:, 1, q])
            nc.gpsimd.tensor_tensor(out=exp_z[:, q], in0=sgn_z[:, q], in1=rec_z[:, q], op=ALU.mult)

        def den_d(b):
            nc.vector.tensor_tensor_scan(
                out=trans[:, b * NB + 1 : (b + 1) * NB + 1],
                data0=pow_u[:, batch(b)],
                data1=exp_z[:, batch(b)],
                initial=trans[:, b * NB : b * NB + 1],
                op0=ALU.mult,
                op1=ALU.mult,
            )

        def den_w(b):
            nc.vector.tensor_tensor(
                out=wgt[:, batch(b)],
                in0=trans[:, batch(b)],
                in1=trans[:, b * NB + 1 : (b + 1) * NB + 1],
                op=ALU.subtract,
            )

        def o_mm(s, c):
            o_ps[s, c] = bank([P, CG], F32, "o_ps")
            for gi in range(G):
                out_mm(o_ps[s, c][:], s, gi, c, CG)

        def sig(s, c):
            sgm[s, c] = work.tile([P, CG], F32, name="sgm", bufs=12)
            nc.scalar.activation(out=sgm[s, c][:], in_=o_ps[s, c][:], func=ACT.Sigmoid)

        acc = {}

        def comp(s, c, c0, c1):
            if c0 == 0:
                acc[s, c] = work.tile([P, CG], F32, name="acc%d" % c, bufs=3)
            if s == 0:
                nc.vector.tensor_scalar(
                    out=acc[s, c][:, c0:c1], in0=sgm[s, c][:, c0:c1], scalar1=wgt[:, s : s + 1], scalar2=None, op0=ALU.mult
                )
            else:
                nc.vector.scalar_tensor_tensor(
                    out=acc[s, c][:, c0:c1],
                    in0=sgm[s, c][:, c0:c1],
                    scalar=wgt[:, s : s + 1],
                    in1=acc[s - 1, c][:, c0:c1],
                    op0=ALU.mult,
                    op1=ALU.add,
                )
            if s == S - 1:
                nc.sync.dma_start(out=out[:, c * CG + c0 : c * CG + c1], in_=acc[s, c][:, c0:c1])

        pos_place()
        freq_lay()
        for h in range(2):
            pos_turn(h)
        for h in range(2):
            pos_copy(h)
        for s in range(8):
            phase_mm(s)
        def encode_s(j):
            encode_abs(2 * j)
            encode_abs(2 * j + 1)
            encode_sin(j)
        blocks = [(gi, c, h) for gi in range(2) for c in range(2) for h in range(2)]
        pairs = [(s, gi) for s in range(8) for gi in range(2)]
        gates = [(0, 0), (1, 0), (0, 1), (1, 1)] + pairs[4:]
        outs = pairs
        comps = [(s, c, 0, CG) for s in range(6) for c in range(2)]
        comps += [(6, 0, 0, CG), (6, 1, 0, CG // 2), (7, 0, 0, CG), (6, 1, CG // 2, CG), (7, 1, 0, CG // 2), (7, 1, CG // 2, CG)]
        def gate(i):
            mm_a(*gates[i])
            relu(*gates[i])
        encode_s(0)
        w_lay(0, 0, 0, 64)
        w_lay(0, 0, 64, 128)
        w_lay(0, 1, 0, 128)
        w_quant(0, 0)
        widen_v(0, 0)
        w_quant(0, 1)
        widen_v(0, 1)
        encode_s(1)
        encode_mul(0)
        widen_v(0, 2)
        encode_quant(0)
        widen_v(0, 3)
        encode_s(2)
        encode_mul(1)
        w_lay(1, 0, 0, 128)
        gate(0)
        encode_quant(1)
        lay(*blocks[0])
        widen_v(1, 0)
        encode_s(3)
        w_quant(1, 0)
        gate(1)
        lay(*blocks[1])
        widen_v(1, 1)
        widen_s(1, 2)
        lay_copy(*blocks[0])
        lay(*blocks[2])
        widen_s(1, 3)
        lay_copy(*blocks[1])
        encode_mul(2)
        gate(2)
        lay(*blocks[3])
        w_lay(1, 1, 0, 128)
        encode_quant(2)
        lay_copy(*blocks[2])
        gate(3)
        mm_b(*pairs[0])
        mm_b(*pairs[2])
        lay_copy(*blocks[3])
        gate(4)
        lay(*blocks[4])
        encode_mul(3)
        w_quant(1, 1)
        encode_quant(3)
        gate(5)
        lay(*blocks[5])
        lay_copy(*blocks[4])
        mm_b(*pairs[1])
        mm_b(*pairs[3])
        for i in range(16):
            if i + 6 < 16:
                gate(i + 6)
            if i < 3:
                lay_copy(*blocks[i + 5])
            if i + 4 < 16:
                mm_b(*pairs[i + 4])
            if i < 2:
                lay(*blocks[i + 6])
            add(*pairs[i])
            if i % 2 == 0 and i:
                h_quant(i // 2 - 1)
            if i in (1, 3, 4, 6):
                w2_quant(*((0, 0), (0, 1), (1, 0), (1, 1))[(1, 3, 4, 6).index(i)])
            if i == 8:
                u_mm(0)
            if i == 10:
                den_a(0)
                den_b(0)
                den_c(0)
            if i == 13:
                den_r(0)
            if i == 15:
                den_d(0)
            if i >= 10:
                o_mm(*outs[i - 10])
                sig(*outs[i - 10])
        h_quant(7)
        den_w(0)
        u_mm(1)
        for i, piece in enumerate(comps):
            comp(*piece)
            if i == 1:
                den_a(1)
                den_b(1)
                den_c(1)
            if i + 6 < 16:
                o_mm(*outs[i + 6])
                sig(*outs[i + 6])
            if i == 4:
                den_r(1)
            if i == 6:
                den_d(1)
            if i == 7:
                den_w(1)
